import numpy as np
import ml_dtypes

BF16 = ml_dtypes.bfloat16


def bf(x):
    return np.asarray(x, np.float32).astype(BF16)


def f32(x):
    return np.asarray(x, np.float32)


def f64(x):
    return np.asarray(x).astype(np.float64)


def striped(idx):
    return np.tile(idx.reshape(-1, 16).T, (8, 1))


S, K, H, M, N, E, Q = 512, 512, 128, 256, 192, 1, 192


def sigmoid(v):
    return 1.0 / (1.0 + np.exp(-v))


def setup_inputs():
    return {"base": bf(np.random.standard_normal((M, S))), "x": bf(np.random.standard_normal((K, N))), "w": bf(np.random.standard_normal((E, K, H)) / np.sqrt(K)), "b": f32(0.5 * np.random.standard_normal((H, E))), "w2": bf(1.5 * np.random.standard_normal((E, H, M)) / np.sqrt(H)), "offs": striped(np.random.permutation(S)[:N])}


def reference(base, x, w, b, w2, offs):
    idx = offs[:16].T.reshape(-1)
    z = f64(base).copy()
    for e in range(E):
        t = f64(w)[e].T @ f64(x)[:, e * Q : (e + 1) * Q] + f64(b)[:, e : e + 1]
        t = t * sigmoid(t)
        z[:, idx[e * Q : (e + 1) * Q]] += f64(w2)[e].T @ t
    return z

@@ -1,0 +1,65 @@
+import concourse.mybir as mybir
+from concourse.masks import make_identity
+
+P = 128
+K, H, M = 512, 128, 256
+S, N = 512, 192
+KC = K // P
+MB = M // P
+FLOPS = 2 * N * K * H + 2 * N * H * M
+
+BF16, F32, U16 = mybir.dt.bfloat16, mybir.dt.float32, mybir.dt.uint16
+SILU = mybir.ActivationFunctionType.Silu
+
+
+def tile_rows_ffnback_silu_kernel(tc, base, x, w, b, w2, offs, out):
+    nc = tc.nc
+    with (
+        tc.tile_pool(name="held", bufs=1) as held,
+        tc.psum_pool(name="psum", bufs=1) as psum,
+    ):
+        w_t = held.tile([P, KC, H], BF16)
+        x_t = held.tile([P, KC, N], BF16)
+        base_t = held.tile([P, MB, S], BF16)
+        w2_t = held.tile([P, M], BF16)
+        offs_t = held.tile([P, N // 16], U16)
+        b_t = held.tile([P, 1], F32)
+
+        nc.sync.dma_start(w_t[:], w[0, :, :].rearrange("(p c) h -> p c h", p=P))
+        nc.sync.dma_start(x_t[:], x.rearrange("(p c) n -> p c n", p=P))
+        nc.scalar.dma_start(b_t[:], b)
+        nc.sync.dma_start(base_t[:], base.rearrange("(a p) t -> p a t", p=P))
+        nc.sync.dma_start(w2_t[:], w2[0, :, :])
+        nc.sync.dma_start(offs_t[:], offs)
+
+        zeros = held.tile([P, 1], F32)
+        nc.vector.memset(zeros[:], 0.0)
+        early = held.tile([P, 1], F32)
+        nc.scalar.activation(early[:], zeros[:], SILU, bias=zeros[:])
+
+        ident = held.tile([P, P], BF16)
+        make_identity(nc, ident[:])
+
+        hidden = psum.tile([P, N], F32)
+        for c in range(KC):
+            nc.tensor.matmul(hidden[:], w_t[:, c, :], x_t[:, c, :], start=c == 0, stop=c == KC - 1)
+        h_t = held.tile([P, N], BF16)
+        nc.scalar.activation(h_t[:], hidden[:], SILU, bias=b_t[:])
+
+        windows = [psum.tile([P, S], F32, name=f"window{a}") for a in range(MB)]
+        for a in range(MB):
+            nc.tensor.matmul(windows[a][:], ident[:], base_t[:, a, :], start=True, stop=False)
+        for a in range(MB):
+            nc.tensor.matmul(
+                windows[a][:].indirect(offs_t[:]),
+                w2_t[:, a * P : (a + 1) * P],
+                h_t[:],
+                start=False,
+                stop=True,
+            )
+
+        out_t = [held.tile([P, S], F32, name=f"out_t{a}") for a in range(MB)]
+        nc.vector.tensor_copy(out_t[0][:], windows[0][:])
+        nc.sync.dma_start(out[0:P, :], out_t[0][:])
+        nc.scalar.copy(out_t[1][:], windows[1][:])
+        nc.scalar.dma_start(out[P:M, :], out_t[1][:])

@@ -6,6 +6,7 @@ K, H, M = 512, 128, 256
 S, N = 512, 192
 KC = K // P
 MB = M // P
+WARM_UPS = 4
 FLOPS = 2 * N * K * H + 2 * N * H * M
 
 BF16, F32, U16 = mybir.dt.bfloat16, mybir.dt.float32, mybir.dt.uint16
@@ -39,6 +40,12 @@ def tile_rows_ffnback_silu_kernel(tc, base, x, w, b, w2, offs, out):
 
         ident = held.tile([P, P], BF16)
         make_identity(nc, ident[:])
+
+        cold = held.tile([P, S], BF16)
+        nc.vector.memset(cold[:], 0.0)
+        spare = psum.tile([P, S], F32)
+        for i in range(WARM_UPS):
+            nc.tensor.matmul(spare[:], cold[:, 0:P], cold[:], start=True, stop=True)
 
         hidden = psum.tile([P, N], F32)
         for c in range(KC):

import concourse.mybir as mybir
from concourse.masks import make_identity

P = 128
K, H, M = 512, 128, 256
S, N = 512, 192
KC = K // P
MB = M // P
WARM_UPS = 4
FLOPS = 2 * N * K * H + 2 * N * H * M

BF16, F32, U16 = mybir.dt.bfloat16, mybir.dt.float32, mybir.dt.uint16
SILU = mybir.ActivationFunctionType.Silu


def tile_rows_ffnback_silu_kernel(tc, base, x, w, b, w2, offs, out):
    nc = tc.nc
    with (
        tc.tile_pool(name="held", bufs=1) as held,
        tc.psum_pool(name="psum", bufs=1) as psum,
    ):
        w_t = held.tile([P, KC, H], BF16)
        x_t = held.tile([P, KC, N], BF16)
        base_t = held.tile([P, MB, S], BF16)
        w2_t = held.tile([P, M], BF16)
        offs_t = held.tile([P, N // 16], U16)
        b_t = held.tile([P, 1], F32)

        nc.sync.dma_start(w_t[:], w[0, :, :].rearrange("(p c) h -> p c h", p=P))
        nc.sync.dma_start(x_t[:], x.rearrange("(p c) n -> p c n", p=P))
        nc.scalar.dma_start(b_t[:], b)
        nc.sync.dma_start(base_t[:], base.rearrange("(a p) t -> p a t", p=P))
        nc.sync.dma_start(w2_t[:], w2[0, :, :])
        nc.sync.dma_start(offs_t[:], offs)

        zeros = held.tile([P, 1], F32)
        nc.vector.memset(zeros[:], 0.0)
        early = held.tile([P, 1], F32)
        nc.scalar.activation(early[:], zeros[:], SILU, bias=zeros[:])

        ident = held.tile([P, P], BF16)
        make_identity(nc, ident[:])

        cold = held.tile([P, S], BF16)
        nc.vector.memset(cold[:], 0.0)
        spare = psum.tile([P, S], F32)
        for i in range(WARM_UPS):
            nc.tensor.matmul(spare[:], cold[:, 0:P], cold[:], start=True, stop=True)

        hidden = psum.tile([P, N], F32)
        for c in range(KC):
            nc.tensor.matmul(hidden[:], w_t[:, c, :], x_t[:, c, :], start=c == 0, stop=c == KC - 1)
        h_t = held.tile([P, N], BF16)
        nc.scalar.activation(h_t[:], hidden[:], SILU, bias=b_t[:])

        windows = [psum.tile([P, S], F32, name=f"window{a}") for a in range(MB)]
        for a in range(MB):
            nc.tensor.matmul(windows[a][:], ident[:], base_t[:, a, :], start=True, stop=False)
        for a in range(MB):
            nc.tensor.matmul(
                windows[a][:].indirect(offs_t[:]),
                w2_t[:, a * P : (a + 1) * P],
                h_t[:],
                start=False,
                stop=True,
            )

        out_t = [held.tile([P, S], F32, name=f"out_t{a}") for a in range(MB)]
        nc.vector.tensor_copy(out_t[0][:], windows[0][:])
        nc.sync.dma_start(out[0:P, :], out_t[0][:])
        nc.scalar.copy(out_t[1][:], windows[1][:])
        nc.scalar.dma_start(out[P:M, :], out_t[1][:])
